import numpy as np
import ml_dtypes


def mxq(x, axis, fmt="e4m3"):
    dtype, down = {"e4m3": (ml_dtypes.float8_e4m3fn, 7), "e5m2": (ml_dtypes.float8_e5m2, 14)}[fmt]
    v = np.moveaxis(np.asarray(x, np.float32).astype(ml_dtypes.bfloat16).astype(np.float64), axis, -1)
    blocks = v.reshape(v.shape[:-1] + (-1, 32))
    amax = np.abs(blocks).max(-1, keepdims=True)
    byte = np.maximum(np.where(amax > 0, np.frexp(amax)[1] - 1 + 127, 0) - down, 1)
    scale = np.exp2(byte - 127.0)
    codes = (blocks / scale).astype(np.float32).astype(dtype).astype(np.float64)
    return np.moveaxis((codes * scale).reshape(v.shape), -1, axis)


WIDE = False


def mx_kscale(k):
    if not WIDE:
        return np.ones(k)
    levels = np.array([10, -10, 5, -5, 0])
    if k % 512:
        return np.exp2(np.random.permutation(np.resize(levels, k // 32))).repeat(32)
    a = np.empty((k // 512, 16))
    for p in range(k // 512):
        a[p, :8] = np.random.permutation(np.resize(levels, 8))
        for g in range(8):
            far = levels[np.abs(levels - a[p, g]) >= 10]
            a[p, g + 8] = far[np.random.randint(len(far))]
    return np.exp2(a.ravel()).repeat(32)


def f64(x):
    return np.asarray(x).astype(np.float64)


def striped(idx):
    return np.tile(idx.reshape(-1, 16).T, (8, 1)).astype(np.uint16)


def unstriped(offs):
    return offs[:16].T.reshape(-1).astype(np.int64)


E2M1 = np.array([0.0, 0.5, 1.0, 1.5, 2.0, 3.0, 4.0, 6.0, -0.0, -0.5, -1.0, -1.5, -2.0, -3.0, -4.0, -6.0])


def pack_weight(w, fmt):
    k, n = w.shape
    w = f64(np.asarray(w, np.float32).astype(ml_dtypes.bfloat16)).reshape(k // 32, 32, n)
    amax = np.abs(w).max(1)
    if fmt == "e4m3":
        byte = np.frexp(amax)[1] - 1 + 127 - 7
    else:
        mant, ex = np.frexp(amax / 6.0)
        byte = np.where(mant > 0.5, ex, ex - 1) + 127
    byte = np.clip(np.where(amax > 0, byte, 1), 1, 254)
    scaled = (w * np.exp2(127.0 - byte)[:, None, :]).reshape(k, n).astype(np.float32)
    by_word = np.ascontiguousarray(scaled.reshape(k // 512, 128, 4, n).transpose(0, 1, 3, 2))
    if fmt == "e4m3":
        words = by_word.astype(ml_dtypes.float8_e4m3fn).view(np.uint8)
    else:
        c = by_word.astype(ml_dtypes.float4_e2m1fn).view(np.uint8) & 0xF
        words = (c[..., 0::2] | (c[..., 1::2] << 4)).reshape(k // 512, 128, 2 * n)
    return np.ascontiguousarray(words), np.ascontiguousarray(byte.astype(np.uint8).reshape(k // 512, 16, n))


def unpack_weight(words, scales, fmt):
    g, _, n = scales.shape
    words = np.ascontiguousarray(words).reshape(g, 128, n, -1)
    if fmt == "e4m3":
        vals = words.view(ml_dtypes.float8_e4m3fn).astype(np.float64)
    else:
        nib = np.empty((g, 128, n, 4), np.uint8)
        nib[..., 0::2] = words & 0xF
        nib[..., 1::2] = words >> 4
        vals = E2M1[nib]
    vals = vals * np.repeat(np.exp2(scales.astype(np.float64) - 127.0), 8, axis=1)[..., None]
    return vals.transpose(0, 1, 3, 2).reshape(g * 512, n)


def gelu(v):
    return 0.5 * v * (1.0 + np.tanh(np.sqrt(2.0 / np.pi) * (v + 0.044715 * v**3)))


def bf(x):
    return np.asarray(x, np.float32).astype(ml_dtypes.bfloat16)


def planes(Y):
    n, m = Y.shape
    b = f64(bf(Y)).reshape(n // 32, 32, m)
    amax = np.abs(b).max(1)
    byte = np.clip(np.where(amax > 0, np.frexp(amax)[1] - 1 + 127 - 7, 1), 1, 254)
    codes = (b * np.exp2(127.0 - byte)[:, None, :]).reshape(n, m).astype(np.float32).astype(ml_dtypes.float8_e4m3fn).view(np.uint8)
    words = codes.reshape(n // 512, 128, 4, m).transpose(0, 1, 3, 2)
    return np.ascontiguousarray(words), np.ascontiguousarray(byte.astype(np.uint8).reshape(n // 512, 16, m))


K, H, N, T, S = 1024, 1024, 1024, 4096, 512

def setup_inputs():
    n = np.random.standard_normal
    s = mx_kscale(K)[:, None]
    u = mx_kscale(H)[:, None]
    tab_words, tab_scales = pack_weight(n((K, T)) * s, "e4m3")
    w2_words, w2_scales = pack_weight(0.45 * n((K, H)) / np.sqrt(K) / s, "e4m3")
    w4 = n((H, N)) / np.sqrt(H) * np.exp(0.8 * n(N))[None, :]
    w4_words, w4_scales = pack_weight(w4 / u, "e2m1")
    return {
        "tab_words": tab_words, "tab_scales": tab_scales,
        "offs": striped(np.random.permutation(T)[:S]),
        "offs2": striped(np.random.permutation(T)[:S]),
        "offs3": striped(np.random.permutation(T)[:S]),
        "w1": (n((K, H)) / np.sqrt(K) / s * u.T).astype(np.float32),
        "w2_words": w2_words, "w2_scales": w2_scales,
        "b2": np.random.uniform(-0.5, 0.5, H).astype(np.float32),
        "w3": (n((K, H)) / np.sqrt(K) / s * u.T).astype(np.float32),
        "w4_words": w4_words, "w4_scales": w4_scales,
    }

def reference(tab_words, tab_scales, offs, offs2, offs3, w1, w2_words, w2_scales, b2, w3, w4_words, w4_scales):
    TW = unpack_weight(tab_words, tab_scales, "e4m3")
    v = TW[:, unstriped(offs)]
    v2 = TW[:, unstriped(offs2)]
    v3 = TW[:, unstriped(offs3)]
    w2 = unpack_weight(w2_words, w2_scales, "e4m3")
    w4 = unpack_weight(w4_words, w4_scales, "e2m1")
    idiom = mxq(f64(w1), 0, "e4m3").T @ v
    phrasing = (w2.T @ v2) + f64(b2)[:, None]
    gloss = mxq(f64(w3), 0, "e4m3").T @ v3
    h = idiom * np.cos(phrasing) + np.maximum(idiom, gloss)
    y = w4.T @ mxq(h, 0, "e4m3")
    words, scales = planes(y)
    return y, words, scales

@@ -1,0 +1,267 @@
+from contextlib import ExitStack
+
+import concourse.mybir as mybir
+
+K, H, N, T, S = 1024, 1024, 1024, 4096, 512
+FLOPS = 2 * S * (3 * K * H + H * N)
+
+F32 = mybir.dt.float32
+BF16 = mybir.dt.bfloat16
+I32 = mybir.dt.int32
+U32 = mybir.dt.uint32
+U16 = mybir.dt.uint16
+U8 = mybir.dt.uint8
+FP8X4 = mybir.dt.float8_e4m3fn_x4
+FP4X4 = mybir.dt.float4_e2m1fn_x4
+ALU = mybir.AluOpType
+ACT = mybir.ActivationFunctionType
+
+P = 128
+PACK = 4
+GROUP = P * PACK
+HALF = S // 2
+SQRT2 = 2.0**0.5
+ROUNDED_ON_VECTOR = (("idiom", 0, 0), ("idiom", 0, 1), ("gloss", 0, 0), ("gloss", 0, 1), ("idiom", 1, 0))
+
+
+def tile_list_idiom_rendering_features_kernel(
+    tc, tab_words, tab_scales, offs, offs2, offs3, w1, w2_words, w2_scales, b2, w3, w4_words, w4_scales,
+    out_0, out_1, out_2,
+):
+    nc = tc.nc
+    with ExitStack() as ctx:
+        lists = ctx.enter_context(tc.tile_pool(name="lists", bufs=1))
+        keep = ctx.enter_context(tc.tile_pool(name="keep", bufs=1))
+        psum = ctx.enter_context(tc.psum_pool(name="psum", bufs=1))
+
+        def held(name, shape, dtype, tag=None):
+            return keep.tile(shape, dtype, name=name, tag=tag or name, align_bytes=64)
+
+        def bank(number, shape):
+            return psum.tile(shape, F32, name="bank%d" % number, tag="bank%d" % number)
+
+        tab_plane = held("tab_plane", [P, T], U8)
+        w2_plane_raw = held("w2_plane_raw", [P, H], U8)
+        w4_plane_raw = held("w4_plane_raw", [P, 2, N], U8)
+        nc.vector.memset(tab_plane[:].bitcast(I32), 0)
+        nc.gpsimd.memset(w2_plane_raw[:].bitcast(I32), 0)
+        nc.gpsimd.memset(w4_plane_raw[:].rearrange("p a c -> p (a c)").bitcast(I32), 0)
+
+        list_tiles = {}
+        for name, source in (("phrasing", offs2), ("idiom", offs), ("gloss", offs3)):
+            list_tiles[name] = lists.tile([P, S // 16], U16, name="list_" + name)
+            nc.sync.dma_start(list_tiles[name][:], source)
+        tab = [held("tab%d" % a, [P, T], U32) for a in range(2)]
+
+        def load_tab(a, first, last):
+            words = tab_words[a].rearrange("p t i -> p (t i)").bitcast(I32)
+            nc.sync.dma_start(tab[a][:, first:last].bitcast(I32), words[:, first:last])
+
+        bias = held("bias", [P, 2, PACK], F32)
+        nc.sync.dma_start(bias[:], b2.rearrange("(b p t) -> p b t", b=2, t=PACK))
+        for part in range(4):
+            load_tab(0, 512 * part, 512 * (part + 1))
+        for q in range(4):
+            nc.sync.dma_start(
+                tab_plane[32 * q : 32 * q + 8, :].bitcast(I32), tab_scales[:, 4 * q : 4 * q + 4, :].bitcast(I32)
+            )
+        w2_raw = [held("w2_raw%d" % b, [P, 2, GROUP], U32) for b in range(2)]
+        w2_view = w2_words.rearrange("a p c i -> p a (c i)").bitcast(I32)
+        w4_raw = held("w4_raw", [P, 2, 2 * N], U8)
+        raw = {}
+
+        def load_w2(b):
+            nc.sync.dma_start(w2_raw[b][:].bitcast(I32), w2_view[:, :, GROUP * b : GROUP * (b + 1)])
+
+        def load_weight(name, source, b):
+            for a in range(2):
+                raw[name, b, a] = held("raw_%s%d%d" % (name, b, a), [P, PACK, GROUP], F32)
+                rows = source[GROUP * a : GROUP * (a + 1), GROUP * b : GROUP * (b + 1)]
+                nc.sync.dma_start(raw[name, b, a][:], rows.rearrange("(p j) c -> p j c", j=PACK))
+
+        load_tab(0, T // 2, T)
+        for q in range(4):
+            nc.sync.dma_start(
+                w2_plane_raw[32 * q : 32 * q + 8, :].bitcast(I32), w2_scales[:, 4 * q : 4 * q + 4, :].bitcast(I32)
+            )
+        load_w2(0)
+        load_tab(1, 0, T)
+        load_w2(1)
+        load_weight("idiom", w1, 0)
+        for q in range(4):
+            nc.sync.dma_start(
+                w4_plane_raw[32 * q : 32 * q + 4].bitcast(I32),
+                w4_scales[:, 4 * q : 4 * q + 4, :].rearrange("a r c -> r a c").bitcast(I32),
+            )
+        load_weight("gloss", w3, 0)
+        load_weight("idiom", w1, 1)
+        load_weight("gloss", w3, 1)
+        nc.sync.dma_start(w4_raw[:].bitcast(I32), w4_words.rearrange("a p c -> p a c").bitcast(I32))
+
+        picked, picked_plane = {}, {}
+
+        def pick_words(a):
+            for name in list_tiles:
+                picked[name, a] = held("picked_%s%d" % (name, a), [P, S], U32)
+                nc.vector.tensor_copy(picked[name, a][:], tab[a][:].indirect(list_tiles[name][:]))
+
+        for name in list_tiles:
+            picked_plane[name] = held("plane_" + name, [P, S], U8)
+            nc.vector.tensor_copy(picked_plane[name][:], tab_plane[:].indirect(list_tiles[name][:]))
+        pick_words(0)
+        half_bias = held("half_bias", [P, 2 * PACK], F32)
+        w2_plane = held("w2_plane", [P, H], U8)
+        w4_plane = held("w4_plane", [P, 2, N], U8)
+        nc.vector.tensor_copy(
+            w2_plane[:].rearrange("p (b t m) -> p b t m", b=2, t=PACK),
+            w2_plane_raw[:].rearrange("p (b m t) -> p b t m", b=2, t=PACK),
+        )
+        nc.vector.tensor_scalar(half_bias[:], bias[:].rearrange("p b t -> p (b t)"), 0.5, None, ALU.mult)
+        pick_words(1)
+
+        w2_codes = [held("w2_codes%d" % b, [P, 2, GROUP], U32) for b in range(2)]
+        codes, planes = {}, {}
+        turned, idiom, h_codes, h_plane = {}, {}, {}, {}
+
+        def deal_w2(b):
+            nc.scalar.copy(
+                w2_codes[b][:].rearrange("p a (u e m) -> p a u m e", u=2, e=2),
+                w2_raw[b][:].rearrange("p a (m u e) -> p a u m e", u=2, e=2),
+            )
+
+        def quantise_weight(name, b, a):
+            grouped = keep.tile([P, PACK * GROUP], BF16, name="grouped", tag="grouped", bufs=4, align_bytes=64)
+            copy = nc.vector.tensor_copy if (name, b, a) in ROUNDED_ON_VECTOR else nc.scalar.copy
+            copy(
+                grouped[:].rearrange("p (u e m j) -> p u m j e", u=2, e=2, j=PACK),
+                raw[name, b, a][:].rearrange("p j (m u e) -> p u m j e", u=2, e=2),
+            )
+            codes[name, b, a] = held("codes_%s%d%d" % (name, b, a), [P, GROUP], U32)
+            planes[name, b, a] = held("planes_%s%d%d" % (name, b, a), [P, GROUP], U8)
+            nc.vector.quantize_mx(codes[name, b, a][:].bitcast(FP8X4), planes[name, b, a][:], grouped[:])
+
+        def first_pass(out, name, b, a, t, cols, start, stop):
+            rows = slice(P * t, P * (t + 1))
+            if name == "phrasing":
+                lhs = w2_codes[b][:, a, rows]
+                lhs_scale = w2_plane[4 * a :, GROUP * b + P * t : GROUP * b + P * (t + 1)]
+            else:
+                lhs, lhs_scale = codes[name, b, a][:, rows], planes[name, b, a][:, rows]
+            nc.tensor.matmul_mx(
+                out, lhsT=lhs.bitcast(FP8X4), lhsT_scale=lhs_scale,
+                rhs=picked[name, a][:, cols].bitcast(FP8X4), rhs_scale=picked_plane[name][4 * a :, cols],
+                start=start, stop=stop,
+            )
+
+        def phrasing_stage(b):
+            deal_w2(b)
+            turned[b] = held("turned%d" % b, [P, PACK, S], F32)
+            accs = [bank(PACK * b + t, [P, S]) for t in range(PACK)]
+            for a in range(2):
+                for t in range(PACK):
+                    first_pass(accs[t][:], "phrasing", b, a, t, slice(0, S), a == 0, a == 1)
+            for t in range(PACK):
+                nc.scalar.activation(
+                    turned[b][:, t, :], accs[t][:], ACT.Sin,
+                    bias=half_bias[:, PACK * b + t : PACK * b + t + 1], scale=0.5,
+                )
+
+        def idiom_stage(b):
+            idiom[b] = held("idiom%d" % b, [P, PACK, S], F32)
+            accs = [bank(PACK * b + t, [P, S]) for t in range(PACK)]
+            for a in range(2):
+                quantise_weight("idiom", b, a)
+                for t in range(PACK):
+                    first_pass(accs[t][:], "idiom", b, a, t, slice(0, S), a == 0, a == 1)
+            for t in range(PACK):
+                nc.scalar.copy(idiom[b][:, t, :], accs[t][:])
+
+        def staged(name):
+            return keep.tile([P, PACK * HALF], BF16, name=name, tag="staged", bufs=4, align_bytes=64)
+
+        def join(b, s):
+            cols = slice(HALF * s, HALF * (s + 1))
+            part = turned[b][:, :, cols]
+            nc.scalar.activation(part, part, ACT.Square, scale=SQRT2)
+            nc.vector.scalar_tensor_tensor(part, part, 1.0, idiom[b][:, :, cols], ALU.subtract, ALU.mult)
+            accs = [bank(2 * b + u, [P, 2, HALF]) for u in range(2)]
+            for a in range(2):
+                for t in range(PACK):
+                    first_pass(
+                        accs[t // 2][:, t % 2, :], "gloss", b, a, t, cols, a == 0 and t % 2 == 0, a == 1 and t % 2 == 1
+                    )
+            for u in range(2):
+                larger = idiom[b][:, 2 * u : 2 * u + 2, cols]
+                nc.vector.tensor_tensor(larger, accs[u][:], larger, ALU.max)
+            grouped = staged("h_grouped")
+            nc.vector.tensor_tensor(
+                grouped[:].rearrange("p (c i t) -> p c t i", i=2, t=PACK),
+                idiom[b][:, :, cols].rearrange("p t (c i) -> p c t i", i=2),
+                part.rearrange("p t (c i) -> p c t i", i=2),
+                ALU.subtract,
+            )
+            h_codes[b, s] = held("h_codes%d%d" % (b, s), [P, HALF], U32)
+            h_plane[b, s] = held("h_plane%d%d" % (b, s), [P, HALF], U8)
+            nc.vector.quantize_mx(h_codes[b, s][:].bitcast(FP8X4), h_plane[b, s][:], grouped[:])
+
+        w4_codes = held("w4_codes", [P, 2, 2 * N], U8)
+        y_codes = [held("y_codes%d" % g, [P, S], U32) for g in range(2)]
+        y_plane = held("y_plane", [P, 2, S], U8)
+
+        def second_stage(s):
+            cols = slice(HALF * s, HALF * (s + 1))
+            accs = [bank(4 * (1 - s) + u, [P, 2, HALF]) for u in range(4)]
+            for a in range(2):
+                for tile_n in range(2 * PACK):
+                    first = P * tile_n
+                    nc.tensor.matmul_mx(
+                        accs[tile_n // 2][:, tile_n % 2, :],
+                        lhsT=w4_codes[:, a, 2 * first : 2 * (first + P)].bitcast(FP4X4),
+                        lhsT_scale=w4_plane[:, a, first : first + P],
+                        rhs=h_codes[a, s][:].bitcast(FP8X4), rhs_scale=h_plane[a, s][:],
+                        start=(a == 0 and tile_n % 2 == 0), stop=(a == 1 and tile_n % 2 == 1),
+                    )
+            for g in range(2):
+                y = held("y%d%d" % (g, s), [P, PACK, HALF], F32, tag="raw_%s0%d" % (("idiom", "gloss")[s], g))
+                for u in range(2):
+                    copy = nc.vector.tensor_copy if (s, g, u) == (1, 0, 1) else nc.scalar.copy
+                    copy(y[:, 2 * u : 2 * u + 2, :], accs[2 * g + u][:])
+                nc.sync.dma_start(
+                    out_0[GROUP * g : GROUP * (g + 1), cols].rearrange("(p t) j -> p t j", t=PACK), y[:]
+                )
+                grouped = staged("y_grouped")
+                copy = nc.scalar.copy if (s, g) == (0, 0) else nc.vector.tensor_copy
+                copy(
+                    grouped[:].rearrange("p (c i t) -> p c t i", i=2, t=PACK),
+                    y[:].rearrange("p t (c i) -> p c t i", i=2),
+                )
+                nc.vector.quantize_mx(y_codes[g][:, cols].bitcast(FP8X4), y_plane[:, g, cols], grouped[:])
+                nc.sync.dma_start(
+                    out_1[g].rearrange("p m i -> p (m i)").bitcast(I32)[:, cols], y_codes[g][:, cols].bitcast(I32)
+                )
+
+        for b in range(2):
+            phrasing_stage(b)
+        for b in range(2):
+            idiom_stage(b)
+            for a in range(2):
+                quantise_weight("gloss", b, a)
+        for s in range(2):
+            for b in range(2):
+                join(b, s)
+            if s == 0:
+                nc.vector.tensor_copy(
+                    w4_plane[:].rearrange("p a (g t m) -> p (a g) t m", g=2, t=PACK),
+                    w4_plane_raw[:].rearrange("p a (g m t) -> p (a g) t m", g=2, t=PACK),
+                )
+                nc.scalar.copy(
+                    w4_codes[:].bitcast(U16).rearrange("p a (g t m) -> p (a g) t m", g=2, t=PACK),
+                    w4_raw[:].bitcast(U16).rearrange("p a (g m t) -> p (a g) t m", g=2, t=PACK),
+                )
+            second_stage(s)
+        for q in range(4):
+            queue = nc.sync if q % 2 == 0 else nc.scalar
+            queue.dma_start(
+                out_2[:, 4 * q : 4 * q + 4, :].rearrange("g r m -> r g m").bitcast(I32),
+                y_plane[32 * q : 32 * q + 4].bitcast(I32),
+            )

@@ -155,35 +155,35 @@ def tile_list_idiom_rendering_features_kernel(
 
         def phrasing_stage(b):
             deal_w2(b)
-            turned[b] = held("turned%d" % b, [P, PACK, S], F32)
+            turned[b] = held("turned%d" % b, [P, 2, PACK, HALF], F32)
             accs = [bank(PACK * b + t, [P, S]) for t in range(PACK)]
             for a in range(2):
                 for t in range(PACK):
                     first_pass(accs[t][:], "phrasing", b, a, t, slice(0, S), a == 0, a == 1)
             for t in range(PACK):
                 nc.scalar.activation(
-                    turned[b][:, t, :], accs[t][:], ACT.Sin,
+                    turned[b][:, :, t, :], accs[t][:].rearrange("p (s j) -> p s j", s=2), ACT.Sin,
                     bias=half_bias[:, PACK * b + t : PACK * b + t + 1], scale=0.5,
                 )
 
         def idiom_stage(b):
-            idiom[b] = held("idiom%d" % b, [P, PACK, S], F32)
+            idiom[b] = held("idiom%d" % b, [P, 2, PACK, HALF], F32)
             accs = [bank(PACK * b + t, [P, S]) for t in range(PACK)]
             for a in range(2):
                 quantise_weight("idiom", b, a)
                 for t in range(PACK):
                     first_pass(accs[t][:], "idiom", b, a, t, slice(0, S), a == 0, a == 1)
             for t in range(PACK):
-                nc.scalar.copy(idiom[b][:, t, :], accs[t][:])
+                nc.scalar.copy(idiom[b][:, :, t, :], accs[t][:].rearrange("p (s j) -> p s j", s=2))
 
-        def staged(name):
-            return keep.tile([P, PACK * HALF], BF16, name=name, tag="staged", bufs=4, align_bytes=64)
+        h_grouped = held("h_grouped", [P, 4, PACK * HALF], BF16, tag="tab0")
+        y_grouped = held("y_grouped", [P, 4, PACK * HALF], BF16, tag="tab1")
 
         def join(b, s):
             cols = slice(HALF * s, HALF * (s + 1))
-            part = turned[b][:, :, cols]
+            part = turned[b][:, s]
             nc.scalar.activation(part, part, ACT.Square, scale=SQRT2)
-            nc.vector.scalar_tensor_tensor(part, part, 1.0, idiom[b][:, :, cols], ALU.subtract, ALU.mult)
+            nc.vector.scalar_tensor_tensor(part, part, 1.0, idiom[b][:, s], ALU.subtract, ALU.mult)
             accs = [bank(2 * b + u, [P, 2, HALF]) for u in range(2)]
             for a in range(2):
                 for t in range(PACK):
@@ -191,18 +191,18 @@ def tile_list_idiom_rendering_features_kernel(
                         accs[t // 2][:, t % 2, :], "gloss", b, a, t, cols, a == 0 and t % 2 == 0, a == 1 and t % 2 == 1
                     )
             for u in range(2):
-                larger = idiom[b][:, 2 * u : 2 * u + 2, cols]
+                larger = idiom[b][:, s, 2 * u : 2 * u + 2, :]
                 nc.vector.tensor_tensor(larger, accs[u][:], larger, ALU.max)
-            grouped = staged("h_grouped")
+            grouped = h_grouped[:, 2 * s + b, :]
             nc.vector.tensor_tensor(
-                grouped[:].rearrange("p (c i t) -> p c t i", i=2, t=PACK),
-                idiom[b][:, :, cols].rearrange("p t (c i) -> p c t i", i=2),
+                grouped.rearrange("p (c i t) -> p c t i", i=2, t=PACK),
+                idiom[b][:, s].rearrange("p t (c i) -> p c t i", i=2),
                 part.rearrange("p t (c i) -> p c t i", i=2),
                 ALU.subtract,
             )
             h_codes[b, s] = held("h_codes%d%d" % (b, s), [P, HALF], U32)
             h_plane[b, s] = held("h_plane%d%d" % (b, s), [P, HALF], U8)
-            nc.vector.quantize_mx(h_codes[b, s][:].bitcast(FP8X4), h_plane[b, s][:], grouped[:])
+            nc.vector.quantize_mx(h_codes[b, s][:].bitcast(FP8X4), h_plane[b, s][:], grouped)
 
         w4_codes = held("w4_codes", [P, 2, 2 * N], U8)
         y_codes = [held("y_codes%d" % g, [P, S], U32) for g in range(2)]
@@ -229,13 +229,12 @@ def tile_list_idiom_rendering_features_kernel(
                 nc.sync.dma_start(
                     out_0[GROUP * g : GROUP * (g + 1), cols].rearrange("(p t) j -> p t j", t=PACK), y[:]
                 )
-                grouped = staged("y_grouped")
-                copy = nc.scalar.copy if (s, g) == (0, 0) else nc.vector.tensor_copy
-                copy(
-                    grouped[:].rearrange("p (c i t) -> p c t i", i=2, t=PACK),
+                grouped = y_grouped[:, 2 * s + g, :]
+                nc.vector.tensor_copy(
+                    grouped.rearrange("p (c i t) -> p c t i", i=2, t=PACK),
                     y[:].rearrange("p t (c i) -> p c t i", i=2),
                 )
-                nc.vector.quantize_mx(y_codes[g][:, cols].bitcast(FP8X4), y_plane[:, g, cols], grouped[:])
+                nc.vector.quantize_mx(y_codes[g][:, cols].bitcast(FP8X4), y_plane[:, g, cols], grouped)
                 nc.sync.dma_start(
                     out_1[g].rearrange("p m i -> p (m i)").bitcast(I32)[:, cols], y_codes[g][:, cols].bitcast(I32)
                 )

@@ -21,7 +21,7 @@ PACK = 4
 GROUP = P * PACK
 HALF = S // 2
 SQRT2 = 2.0**0.5
-ROUNDED_ON_VECTOR = (("idiom", 0, 0), ("idiom", 0, 1), ("gloss", 0, 0), ("gloss", 0, 1), ("idiom", 1, 0))
+ROUNDED_ON_VECTOR = (("idiom", 0, 0), ("idiom", 0, 1), ("gloss", 0, 0), ("gloss", 0, 1), ("gloss", 1, 1))
 
 
 def tile_list_idiom_rendering_features_kernel(
@@ -131,11 +131,13 @@ def tile_list_idiom_rendering_features_kernel(
 
         def quantise_weight(name, b, a):
             grouped = keep.tile([P, PACK * GROUP], BF16, name="grouped", tag="grouped", bufs=4, align_bytes=64)
-            copy = nc.vector.tensor_copy if (name, b, a) in ROUNDED_ON_VECTOR else nc.scalar.copy
-            copy(
-                grouped[:].rearrange("p (u e m j) -> p u m j e", u=2, e=2, j=PACK),
-                raw[name, b, a][:].rearrange("p j (m u e) -> p u m j e", u=2, e=2),
-            )
+            dealt = grouped[:].rearrange("p (u e m j) -> p u m j e", u=2, e=2, j=PACK)
+            source = raw[name, b, a][:].rearrange("p j (m u e) -> p u m j e", u=2, e=2)
+            if (name, b, a) in ROUNDED_ON_VECTOR:
+                for u in range(2):
+                    nc.vector.tensor_copy(dealt[:, u], source[:, u])
+            else:
+                nc.scalar.copy(dealt, source)
             codes[name, b, a] = held("codes_%s%d%d" % (name, b, a), [P, GROUP], U32)
             planes[name, b, a] = held("planes_%s%d%d" % (name, b, a), [P, GROUP], U8)
             nc.vector.quantize_mx(codes[name, b, a][:].bitcast(FP8X4), planes[name, b, a][:], grouped[:])
@@ -224,8 +226,7 @@ def tile_list_idiom_rendering_features_kernel(
             for g in range(2):
                 y = held("y%d%d" % (g, s), [P, PACK, HALF], F32, tag="raw_%s0%d" % (("idiom", "gloss")[s], g))
                 for u in range(2):
-                    copy = nc.vector.tensor_copy if (s, g, u) == (1, 0, 1) else nc.scalar.copy
-                    copy(y[:, 2 * u : 2 * u + 2, :], accs[2 * g + u][:])
+                    nc.scalar.copy(y[:, 2 * u : 2 * u + 2, :], accs[2 * g + u][:])
                 nc.sync.dma_start(
                     out_0[GROUP * g : GROUP * (g + 1), cols].rearrange("(p t) j -> p t j", t=PACK), y[:]
                 )

@@ -73,11 +73,10 @@ def tile_list_idiom_rendering_features_kernel(
         def load_w2(b):
             nc.sync.dma_start(w2_raw[b][:].bitcast(I32), w2_view[:, :, GROUP * b : GROUP * (b + 1)])
 
-        def load_weight(name, source, b):
-            for a in range(2):
-                raw[name, b, a] = held("raw_%s%d%d" % (name, b, a), [P, PACK, GROUP], F32)
-                rows = source[GROUP * a : GROUP * (a + 1), GROUP * b : GROUP * (b + 1)]
-                nc.sync.dma_start(raw[name, b, a][:], rows.rearrange("(p j) c -> p j c", j=PACK))
+        def load_weight(name, b, a):
+            raw[name, b, a] = held("raw_%s%d%d" % (name, b, a), [P, PACK, GROUP], F32)
+            rows = {"idiom": w1, "gloss": w3}[name][GROUP * a : GROUP * (a + 1), GROUP * b : GROUP * (b + 1)]
+            nc.sync.dma_start(raw[name, b, a][:], rows.rearrange("(p j) c -> p j c", j=PACK))
 
         load_tab(0, T // 2, T)
         for q in range(4):
@@ -86,17 +85,18 @@ def tile_list_idiom_rendering_features_kernel(
             )
         load_w2(0)
         load_tab(1, 0, T)
+        load_weight("idiom", 0, 0)
         load_w2(1)
-        load_weight("idiom", w1, 0)
+        load_weight("idiom", 0, 1)
         for q in range(4):
             nc.sync.dma_start(
                 w4_plane_raw[32 * q : 32 * q + 4].bitcast(I32),
                 w4_scales[:, 4 * q : 4 * q + 4, :].rearrange("a r c -> r a c").bitcast(I32),
             )
-        load_weight("gloss", w3, 0)
-        load_weight("idiom", w1, 1)
-        load_weight("gloss", w3, 1)
+        for name, b, a in (("gloss", 0, 0), ("gloss", 0, 1), ("idiom", 1, 0), ("idiom", 1, 1), ("gloss", 1, 0)):
+            load_weight(name, b, a)
         nc.sync.dma_start(w4_raw[:].bitcast(I32), w4_words.rearrange("a p c -> p a c").bitcast(I32))
+        load_weight("gloss", 1, 1)
 
         picked, picked_plane = {}, {}
 
@@ -136,6 +136,9 @@ def tile_list_idiom_rendering_features_kernel(
             if (name, b, a) in ROUNDED_ON_VECTOR:
                 for u in range(2):
                     nc.vector.tensor_copy(dealt[:, u], source[:, u])
+            elif (name, b, a) == ("idiom", 1, 0):
+                nc.scalar.copy(dealt[:, 0], source[:, 0])
+                nc.vector.tensor_copy(dealt[:, 1], source[:, 1])
             else:
                 nc.scalar.copy(dealt, source)
             codes[name, b, a] = held("codes_%s%d%d" % (name, b, a), [P, GROUP], U32)

from contextlib import ExitStack

import concourse.mybir as mybir

K, H, N, T, S = 1024, 1024, 1024, 4096, 512
FLOPS = 2 * S * (3 * K * H + H * N)

F32 = mybir.dt.float32
BF16 = mybir.dt.bfloat16
I32 = mybir.dt.int32
U32 = mybir.dt.uint32
U16 = mybir.dt.uint16
U8 = mybir.dt.uint8
FP8X4 = mybir.dt.float8_e4m3fn_x4
FP4X4 = mybir.dt.float4_e2m1fn_x4
ALU = mybir.AluOpType
ACT = mybir.ActivationFunctionType

P = 128
PACK = 4
GROUP = P * PACK
HALF = S // 2
SQRT2 = 2.0**0.5
ROUNDED_ON_VECTOR = (("idiom", 0, 0), ("idiom", 0, 1), ("gloss", 0, 0), ("gloss", 0, 1), ("gloss", 1, 1))


def tile_list_idiom_rendering_features_kernel(
    tc, tab_words, tab_scales, offs, offs2, offs3, w1, w2_words, w2_scales, b2, w3, w4_words, w4_scales,
    out_0, out_1, out_2,
):
    nc = tc.nc
    with ExitStack() as ctx:
        lists = ctx.enter_context(tc.tile_pool(name="lists", bufs=1))
        keep = ctx.enter_context(tc.tile_pool(name="keep", bufs=1))
        psum = ctx.enter_context(tc.psum_pool(name="psum", bufs=1))

        def held(name, shape, dtype, tag=None):
            return keep.tile(shape, dtype, name=name, tag=tag or name, align_bytes=64)

        def bank(number, shape):
            return psum.tile(shape, F32, name="bank%d" % number, tag="bank%d" % number)

        tab_plane = held("tab_plane", [P, T], U8)
        w2_plane_raw = held("w2_plane_raw", [P, H], U8)
        w4_plane_raw = held("w4_plane_raw", [P, 2, N], U8)
        nc.vector.memset(tab_plane[:].bitcast(I32), 0)
        nc.gpsimd.memset(w2_plane_raw[:].bitcast(I32), 0)
        nc.gpsimd.memset(w4_plane_raw[:].rearrange("p a c -> p (a c)").bitcast(I32), 0)

        list_tiles = {}
        for name, source in (("phrasing", offs2), ("idiom", offs), ("gloss", offs3)):
            list_tiles[name] = lists.tile([P, S // 16], U16, name="list_" + name)
            nc.sync.dma_start(list_tiles[name][:], source)
        tab = [held("tab%d" % a, [P, T], U32) for a in range(2)]

        def load_tab(a, first, last):
            words = tab_words[a].rearrange("p t i -> p (t i)").bitcast(I32)
            nc.sync.dma_start(tab[a][:, first:last].bitcast(I32), words[:, first:last])

        bias = held("bias", [P, 2, PACK], F32)
        nc.sync.dma_start(bias[:], b2.rearrange("(b p t) -> p b t", b=2, t=PACK))
        for part in range(4):
            load_tab(0, 512 * part, 512 * (part + 1))
        for q in range(4):
            nc.sync.dma_start(
                tab_plane[32 * q : 32 * q + 8, :].bitcast(I32), tab_scales[:, 4 * q : 4 * q + 4, :].bitcast(I32)
            )
        w2_raw = [held("w2_raw%d" % b, [P, 2, GROUP], U32) for b in range(2)]
        w2_view = w2_words.rearrange("a p c i -> p a (c i)").bitcast(I32)
        w4_raw = held("w4_raw", [P, 2, 2 * N], U8)
        raw = {}

        def load_w2(b):
            nc.sync.dma_start(w2_raw[b][:].bitcast(I32), w2_view[:, :, GROUP * b : GROUP * (b + 1)])

        def load_weight(name, b, a):
            raw[name, b, a] = held("raw_%s%d%d" % (name, b, a), [P, PACK, GROUP], F32)
            rows = {"idiom": w1, "gloss": w3}[name][GROUP * a : GROUP * (a + 1), GROUP * b : GROUP * (b + 1)]
            nc.sync.dma_start(raw[name, b, a][:], rows.rearrange("(p j) c -> p j c", j=PACK))

        load_tab(0, T // 2, T)
        for q in range(4):
            nc.sync.dma_start(
                w2_plane_raw[32 * q : 32 * q + 8, :].bitcast(I32), w2_scales[:, 4 * q : 4 * q + 4, :].bitcast(I32)
            )
        load_w2(0)
        load_tab(1, 0, T)
        load_weight("idiom", 0, 0)
        load_w2(1)
        load_weight("idiom", 0, 1)
        for q in range(4):
            nc.sync.dma_start(
                w4_plane_raw[32 * q : 32 * q + 4].bitcast(I32),
                w4_scales[:, 4 * q : 4 * q + 4, :].rearrange("a r c -> r a c").bitcast(I32),
            )
        for name, b, a in (("gloss", 0, 0), ("gloss", 0, 1), ("idiom", 1, 0), ("idiom", 1, 1), ("gloss", 1, 0)):
            load_weight(name, b, a)
        nc.sync.dma_start(w4_raw[:].bitcast(I32), w4_words.rearrange("a p c -> p a c").bitcast(I32))
        load_weight("gloss", 1, 1)

        picked, picked_plane = {}, {}

        def pick_words(a):
            for name in list_tiles:
                picked[name, a] = held("picked_%s%d" % (name, a), [P, S], U32)
                nc.vector.tensor_copy(picked[name, a][:], tab[a][:].indirect(list_tiles[name][:]))

        for name in list_tiles:
            picked_plane[name] = held("plane_" + name, [P, S], U8)
            nc.vector.tensor_copy(picked_plane[name][:], tab_plane[:].indirect(list_tiles[name][:]))
        pick_words(0)
        half_bias = held("half_bias", [P, 2 * PACK], F32)
        w2_plane = held("w2_plane", [P, H], U8)
        w4_plane = held("w4_plane", [P, 2, N], U8)
        nc.vector.tensor_copy(
            w2_plane[:].rearrange("p (b t m) -> p b t m", b=2, t=PACK),
            w2_plane_raw[:].rearrange("p (b m t) -> p b t m", b=2, t=PACK),
        )
        nc.vector.tensor_scalar(half_bias[:], bias[:].rearrange("p b t -> p (b t)"), 0.5, None, ALU.mult)
        pick_words(1)

        w2_codes = [held("w2_codes%d" % b, [P, 2, GROUP], U32) for b in range(2)]
        codes, planes = {}, {}
        turned, idiom, h_codes, h_plane = {}, {}, {}, {}

        def deal_w2(b):
            nc.scalar.copy(
                w2_codes[b][:].rearrange("p a (u e m) -> p a u m e", u=2, e=2),
                w2_raw[b][:].rearrange("p a (m u e) -> p a u m e", u=2, e=2),
            )

        def quantise_weight(name, b, a):
            grouped = keep.tile([P, PACK * GROUP], BF16, name="grouped", tag="grouped", bufs=4, align_bytes=64)
            dealt = grouped[:].rearrange("p (u e m j) -> p u m j e", u=2, e=2, j=PACK)
            source = raw[name, b, a][:].rearrange("p j (m u e) -> p u m j e", u=2, e=2)
            if (name, b, a) in ROUNDED_ON_VECTOR:
                for u in range(2):
                    nc.vector.tensor_copy(dealt[:, u], source[:, u])
            elif (name, b, a) == ("idiom", 1, 0):
                nc.scalar.copy(dealt[:, 0], source[:, 0])
                nc.vector.tensor_copy(dealt[:, 1], source[:, 1])
            else:
                nc.scalar.copy(dealt, source)
            codes[name, b, a] = held("codes_%s%d%d" % (name, b, a), [P, GROUP], U32)
            planes[name, b, a] = held("planes_%s%d%d" % (name, b, a), [P, GROUP], U8)
            nc.vector.quantize_mx(codes[name, b, a][:].bitcast(FP8X4), planes[name, b, a][:], grouped[:])

        def first_pass(out, name, b, a, t, cols, start, stop):
            rows = slice(P * t, P * (t + 1))
            if name == "phrasing":
                lhs = w2_codes[b][:, a, rows]
                lhs_scale = w2_plane[4 * a :, GROUP * b + P * t : GROUP * b + P * (t + 1)]
            else:
                lhs, lhs_scale = codes[name, b, a][:, rows], planes[name, b, a][:, rows]
            nc.tensor.matmul_mx(
                out, lhsT=lhs.bitcast(FP8X4), lhsT_scale=lhs_scale,
                rhs=picked[name, a][:, cols].bitcast(FP8X4), rhs_scale=picked_plane[name][4 * a :, cols],
                start=start, stop=stop,
            )

        def phrasing_stage(b):
            deal_w2(b)
            turned[b] = held("turned%d" % b, [P, 2, PACK, HALF], F32)
            accs = [bank(PACK * b + t, [P, S]) for t in range(PACK)]
            for a in range(2):
                for t in range(PACK):
                    first_pass(accs[t][:], "phrasing", b, a, t, slice(0, S), a == 0, a == 1)
            for t in range(PACK):
                nc.scalar.activation(
                    turned[b][:, :, t, :], accs[t][:].rearrange("p (s j) -> p s j", s=2), ACT.Sin,
                    bias=half_bias[:, PACK * b + t : PACK * b + t + 1], scale=0.5,
                )

        def idiom_stage(b):
            idiom[b] = held("idiom%d" % b, [P, 2, PACK, HALF], F32)
            accs = [bank(PACK * b + t, [P, S]) for t in range(PACK)]
            for a in range(2):
                quantise_weight("idiom", b, a)
                for t in range(PACK):
                    first_pass(accs[t][:], "idiom", b, a, t, slice(0, S), a == 0, a == 1)
            for t in range(PACK):
                nc.scalar.copy(idiom[b][:, :, t, :], accs[t][:].rearrange("p (s j) -> p s j", s=2))

        h_grouped = held("h_grouped", [P, 4, PACK * HALF], BF16, tag="tab0")
        y_grouped = held("y_grouped", [P, 4, PACK * HALF], BF16, tag="tab1")

        def join(b, s):
            cols = slice(HALF * s, HALF * (s + 1))
            part = turned[b][:, s]
            nc.scalar.activation(part, part, ACT.Square, scale=SQRT2)
            nc.vector.scalar_tensor_tensor(part, part, 1.0, idiom[b][:, s], ALU.subtract, ALU.mult)
            accs = [bank(2 * b + u, [P, 2, HALF]) for u in range(2)]
            for a in range(2):
                for t in range(PACK):
                    first_pass(
                        accs[t // 2][:, t % 2, :], "gloss", b, a, t, cols, a == 0 and t % 2 == 0, a == 1 and t % 2 == 1
                    )
            for u in range(2):
                larger = idiom[b][:, s, 2 * u : 2 * u + 2, :]
                nc.vector.tensor_tensor(larger, accs[u][:], larger, ALU.max)
            grouped = h_grouped[:, 2 * s + b, :]
            nc.vector.tensor_tensor(
                grouped.rearrange("p (c i t) -> p c t i", i=2, t=PACK),
                idiom[b][:, s].rearrange("p t (c i) -> p c t i", i=2),
                part.rearrange("p t (c i) -> p c t i", i=2),
                ALU.subtract,
            )
            h_codes[b, s] = held("h_codes%d%d" % (b, s), [P, HALF], U32)
            h_plane[b, s] = held("h_plane%d%d" % (b, s), [P, HALF], U8)
            nc.vector.quantize_mx(h_codes[b, s][:].bitcast(FP8X4), h_plane[b, s][:], grouped)

        w4_codes = held("w4_codes", [P, 2, 2 * N], U8)
        y_codes = [held("y_codes%d" % g, [P, S], U32) for g in range(2)]
        y_plane = held("y_plane", [P, 2, S], U8)

        def second_stage(s):
            cols = slice(HALF * s, HALF * (s + 1))
            accs = [bank(4 * (1 - s) + u, [P, 2, HALF]) for u in range(4)]
            for a in range(2):
                for tile_n in range(2 * PACK):
                    first = P * tile_n
                    nc.tensor.matmul_mx(
                        accs[tile_n // 2][:, tile_n % 2, :],
                        lhsT=w4_codes[:, a, 2 * first : 2 * (first + P)].bitcast(FP4X4),
                        lhsT_scale=w4_plane[:, a, first : first + P],
                        rhs=h_codes[a, s][:].bitcast(FP8X4), rhs_scale=h_plane[a, s][:],
                        start=(a == 0 and tile_n % 2 == 0), stop=(a == 1 and tile_n % 2 == 1),
                    )
            for g in range(2):
                y = held("y%d%d" % (g, s), [P, PACK, HALF], F32, tag="raw_%s0%d" % (("idiom", "gloss")[s], g))
                for u in range(2):
                    nc.scalar.copy(y[:, 2 * u : 2 * u + 2, :], accs[2 * g + u][:])
                nc.sync.dma_start(
                    out_0[GROUP * g : GROUP * (g + 1), cols].rearrange("(p t) j -> p t j", t=PACK), y[:]
                )
                grouped = y_grouped[:, 2 * s + g, :]
                nc.vector.tensor_copy(
                    grouped.rearrange("p (c i t) -> p c t i", i=2, t=PACK),
                    y[:].rearrange("p t (c i) -> p c t i", i=2),
                )
                nc.vector.quantize_mx(y_codes[g][:, cols].bitcast(FP8X4), y_plane[:, g, cols], grouped)
                nc.sync.dma_start(
                    out_1[g].rearrange("p m i -> p (m i)").bitcast(I32)[:, cols], y_codes[g][:, cols].bitcast(I32)
                )

        for b in range(2):
            phrasing_stage(b)
        for b in range(2):
            idiom_stage(b)
            for a in range(2):
                quantise_weight("gloss", b, a)
        for s in range(2):
            for b in range(2):
                join(b, s)
            if s == 0:
                nc.vector.tensor_copy(
                    w4_plane[:].rearrange("p a (g t m) -> p (a g) t m", g=2, t=PACK),
                    w4_plane_raw[:].rearrange("p a (g m t) -> p (a g) t m", g=2, t=PACK),
                )
                nc.scalar.copy(
                    w4_codes[:].bitcast(U16).rearrange("p a (g t m) -> p (a g) t m", g=2, t=PACK),
                    w4_raw[:].bitcast(U16).rearrange("p a (g m t) -> p (a g) t m", g=2, t=PACK),
                )
            second_stage(s)
        for q in range(4):
            queue = nc.sync if q % 2 == 0 else nc.scalar
            queue.dma_start(
                out_2[:, 4 * q : 4 * q + 4, :].rearrange("g r m -> r g m").bitcast(I32),
                y_plane[32 * q : 32 * q + 4].bitcast(I32),
            )
